import numpy as np
import ml_dtypes

BF16 = ml_dtypes.bfloat16


def bf(x):
    return np.asarray(x, np.float32).astype(BF16)


def f32(x):
    return np.asarray(x, np.float32)


def f64(x):
    return np.asarray(x).astype(np.float64)


def striped(idx):
    return np.tile(idx.reshape(-1, 16).T, (8, 1))


def rows(idx, k):
    return np.tile(idx, (k, 1))


def look(tab, idx):
    return np.take_along_axis(f64(tab), rows(idx, len(tab)), axis=1)


K, S, V, N, M = 512, 2048, 1536, 1536, 256


def setup_inputs():
    return {"tab": f32(0.5 * np.random.standard_normal((K, S))), "y": f32(np.random.standard_normal((K, V))), "w": bf(np.random.standard_normal((K, M)) / np.sqrt(K)), "b": f32(0.5 * np.random.standard_normal((M, 1))), "offs": striped(np.random.permutation(S)[:N])}


def reference(tab, y, w, b, offs):
    idx = offs[:16].T.reshape(-1)
    t = look(tab, idx)
    x = np.exp(t) * f64(y)
    y = f64(w).T @ x
    return np.maximum(y + f64(b), 0.0)

@@ -1,0 +1,66 @@
+import concourse.mybir as mybir
+
+F32, BF16, U16 = mybir.dt.float32, mybir.dt.bfloat16, mybir.dt.uint16
+ACT, ALU = mybir.ActivationFunctionType, mybir.AluOpType
+
+P = 128
+K, S, N, M = 512, 2048, 1536, 256
+PIECE = 512
+BLOCKS, PIECES, HALVES = K // P, N // PIECE, M // P
+LANES = 16
+
+FLOPS = 2 * K * M * N
+
+
+def tile_lookup_gate_exp_relu_kernel(tc, tab, y, w, b, offs, out):
+    nc = tc.nc
+
+    tab_blocks = tab.rearrange("(p k) s -> k p s", k=BLOCKS)
+    y_blocks = y.rearrange("(p k) n -> k p n", k=BLOCKS)
+    out_halves = out.rearrange("(p h) n -> h p n", h=HALVES)
+
+    with (
+        tc.tile_pool(name="held", bufs=1) as held,
+        tc.psum_pool(name="psum", bufs=1) as psum,
+    ):
+        offsets = held.tile([P, N // LANES], U16, name="offsets")
+        windows = [held.tile([P, S], F32, name=f"window{k}") for k in range(BLOCKS)]
+        streams = [held.tile([P, N], F32, name=f"stream{k}") for k in range(BLOCKS)]
+        weights = held.tile([P, BLOCKS, P, HALVES], BF16, name="weights")
+        bias = held.tile([P, HALVES], F32, name="bias")
+
+        nc.sync.dma_start(offsets[:], offs)
+        nc.sync.dma_start(windows[0][:], tab_blocks[0])
+        nc.sync.dma_start(windows[1][:], tab_blocks[1])
+        nc.sync.dma_start(weights[:], w.rearrange("(p k) (q h) -> p k q h", k=BLOCKS, h=HALVES))
+        nc.sync.dma_start(bias[:], b.rearrange("(p h) one -> p (h one)", h=HALVES))
+        for k in range(BLOCKS):
+            nc.sync.dma_start(streams[k][:], y_blocks[k])
+            if k + 2 < BLOCKS:
+                nc.sync.dma_start(windows[k + 2][:], tab_blocks[k + 2])
+
+        sums = [
+            [psum.tile([P, PIECE], F32, name=f"sum{j}_{h}") for h in range(HALVES)]
+            for j in range(PIECES)
+        ]
+        for k in range(BLOCKS):
+            for j in range(PIECES):
+                columns = slice(j * PIECE, (j + 1) * PIECE)
+                piece_offsets = offsets[:, j * PIECE // LANES : (j + 1) * PIECE // LANES]
+                gate = held.tile([P, PIECE], F32, name=f"gate{k}_{j}")
+                nc.scalar.activation(gate[:], windows[k][:].indirect(piece_offsets), ACT.Exp)
+                x = held.tile([P, PIECE], BF16, name=f"x{k}_{j}")
+                nc.vector.tensor_tensor(x[:], gate[:], streams[k][:, columns], ALU.mult)
+                for h in range(HALVES):
+                    nc.tensor.matmul(
+                        sums[j][h][:], weights[:, k, :, h], x[:], start=k == 0, stop=k == BLOCKS - 1
+                    )
+
+        for j in range(PIECES):
+            columns = slice(j * PIECE, (j + 1) * PIECE)
+            first = held.tile([P, PIECE], F32, name=f"first{j}")
+            nc.vector.tensor_scalar(first[:], sums[j][0][:], bias[:, 0:1], 0.0, ALU.add, ALU.max)
+            nc.sync.dma_start(out_halves[0][:, columns], first[:])
+            second = held.tile([P, PIECE], F32, name=f"second{j}")
+            nc.scalar.activation(second[:], sums[j][1][:], ACT.Relu, bias=bias[:, 1:2])
+            nc.sync.dma_start(out_halves[1][:, columns], second[:])

@@ -29,15 +29,24 @@ def tile_lookup_gate_exp_relu_kernel(tc, tab, y, w, b, offs, out):
         weights = held.tile([P, BLOCKS, P, HALVES], BF16, name="weights")
         bias = held.tile([P, HALVES], F32, name="bias")
 
+        zero = held.tile([P, 1], F32, name="zero")
+        warm = held.tile([P, 1], F32, name="warm")
+        nc.vector.memset(zero[:], 0.0)
+        nc.scalar.activation(warm[:], zero[:], ACT.Exp)
+
         nc.sync.dma_start(offsets[:], offs)
         nc.sync.dma_start(windows[0][:], tab_blocks[0])
         nc.sync.dma_start(windows[1][:], tab_blocks[1])
         nc.sync.dma_start(weights[:], w.rearrange("(p k) (q h) -> p k q h", k=BLOCKS, h=HALVES))
         nc.sync.dma_start(bias[:], b.rearrange("(p h) one -> p (h one)", h=HALVES))
         for k in range(BLOCKS):
-            nc.sync.dma_start(streams[k][:], y_blocks[k])
             if k + 2 < BLOCKS:
+                nc.sync.dma_start(streams[k][:], y_blocks[k])
                 nc.sync.dma_start(windows[k + 2][:], tab_blocks[k + 2])
+            else:
+                for j in range(PIECES):
+                    columns = slice(j * PIECE, (j + 1) * PIECE)
+                    nc.sync.dma_start(streams[k][:, columns], y_blocks[k][:, columns])
 
         sums = [
             [psum.tile([P, PIECE], F32, name=f"sum{j}_{h}") for h in range(HALVES)]

@@ -7,6 +7,10 @@ P = 128
 K, S, N, M = 512, 2048, 1536, 256
 PIECE = 512
 BLOCKS, PIECES, HALVES = K // P, N // PIECE, M // P
+CHUNKS = [slice(j * PIECE, (j + 1) * PIECE) for j in range(PIECES - 1)] + [
+    slice(N - PIECE, N - PIECE // 2),
+    slice(N - PIECE // 2, N),
+]
 LANES = 16
 
 FLOPS = 2 * K * M * N
@@ -26,16 +30,23 @@ def tile_lookup_gate_exp_relu_kernel(tc, tab, y, w, b, offs, out):
         offsets = held.tile([P, N // LANES], U16, name="offsets")
         windows = [held.tile([P, S], F32, name=f"window{k}") for k in range(BLOCKS)]
         streams = [held.tile([P, N], F32, name=f"stream{k}") for k in range(BLOCKS)]
+        gates = [held.tile([P, N], F32, name=f"gate{k}") for k in range(BLOCKS)]
+        xs = [held.tile([P, N], BF16, name=f"x{k}") for k in range(BLOCKS)]
+        results = [held.tile([P, N], F32, name=f"result{h}") for h in range(HALVES)]
         weights = held.tile([P, BLOCKS, P, HALVES], BF16, name="weights")
         bias = held.tile([P, HALVES], F32, name="bias")
+        sums = [
+            [psum.tile([P, c.stop - c.start], F32, name=f"sum{i}_{h}") for h in range(HALVES)]
+            for i, c in enumerate(CHUNKS)
+        ]
 
         zero = held.tile([P, 1], F32, name="zero")
         warm = held.tile([P, 1], F32, name="warm")
         nc.vector.memset(zero[:], 0.0)
         nc.scalar.activation(warm[:], zero[:], ACT.Exp)
 
-        nc.sync.dma_start(offsets[:], offs)
         nc.sync.dma_start(windows[0][:], tab_blocks[0])
+        nc.sync.dma_start(offsets[:], offs)
         nc.sync.dma_start(windows[1][:], tab_blocks[1])
         nc.sync.dma_start(weights[:], w.rearrange("(p k) (q h) -> p k q h", k=BLOCKS, h=HALVES))
         nc.sync.dma_start(bias[:], b.rearrange("(p h) one -> p (h one)", h=HALVES))
@@ -45,31 +56,23 @@ def tile_lookup_gate_exp_relu_kernel(tc, tab, y, w, b, offs, out):
                 nc.sync.dma_start(windows[k + 2][:], tab_blocks[k + 2])
             else:
                 for j in range(PIECES):
-                    columns = slice(j * PIECE, (j + 1) * PIECE)
-                    nc.sync.dma_start(streams[k][:, columns], y_blocks[k][:, columns])
+                    piece = slice(j * PIECE, (j + 1) * PIECE)
+                    nc.sync.dma_start(streams[k][:, piece], y_blocks[k][:, piece])
 
-        sums = [
-            [psum.tile([P, PIECE], F32, name=f"sum{j}_{h}") for h in range(HALVES)]
-            for j in range(PIECES)
-        ]
         for k in range(BLOCKS):
             for j in range(PIECES):
-                columns = slice(j * PIECE, (j + 1) * PIECE)
-                piece_offsets = offsets[:, j * PIECE // LANES : (j + 1) * PIECE // LANES]
-                gate = held.tile([P, PIECE], F32, name=f"gate{k}_{j}")
-                nc.scalar.activation(gate[:], windows[k][:].indirect(piece_offsets), ACT.Exp)
-                x = held.tile([P, PIECE], BF16, name=f"x{k}_{j}")
-                nc.vector.tensor_tensor(x[:], gate[:], streams[k][:, columns], ALU.mult)
+                piece = slice(j * PIECE, (j + 1) * PIECE)
+                piece_offsets = offsets[:, piece.start // LANES : piece.stop // LANES]
+                nc.scalar.activation(gates[k][:, piece], windows[k][:].indirect(piece_offsets), ACT.Exp)
+            for i, chunk in enumerate(CHUNKS):
+                nc.vector.tensor_tensor(xs[k][:, chunk], gates[k][:, chunk], streams[k][:, chunk], ALU.mult)
                 for h in range(HALVES):
                     nc.tensor.matmul(
-                        sums[j][h][:], weights[:, k, :, h], x[:], start=k == 0, stop=k == BLOCKS - 1
+                        sums[i][h][:], weights[:, k, :, h], xs[k][:, chunk], start=k == 0, stop=k == BLOCKS - 1
                     )
 
-        for j in range(PIECES):
-            columns = slice(j * PIECE, (j + 1) * PIECE)
-            first = held.tile([P, PIECE], F32, name=f"first{j}")
-            nc.vector.tensor_scalar(first[:], sums[j][0][:], bias[:, 0:1], 0.0, ALU.add, ALU.max)
-            nc.sync.dma_start(out_halves[0][:, columns], first[:])
-            second = held.tile([P, PIECE], F32, name=f"second{j}")
-            nc.scalar.activation(second[:], sums[j][1][:], ACT.Relu, bias=bias[:, 1:2])
-            nc.sync.dma_start(out_halves[1][:, columns], second[:])
+        for i, chunk in enumerate(CHUNKS):
+            nc.vector.tensor_scalar(results[0][:, chunk], sums[i][0][:], bias[:, 0:1], 0.0, ALU.add, ALU.max)
+            nc.sync.dma_start(out_halves[0][:, chunk], results[0][:, chunk])
+            nc.scalar.activation(results[1][:, chunk], sums[i][1][:], ACT.Relu, bias=bias[:, 1:2])
+            nc.sync.dma_start(out_halves[1][:, chunk], results[1][:, chunk])

import concourse.mybir as mybir

F32, BF16, U16 = mybir.dt.float32, mybir.dt.bfloat16, mybir.dt.uint16
ACT, ALU = mybir.ActivationFunctionType, mybir.AluOpType

P = 128
K, S, N, M = 512, 2048, 1536, 256
PIECE = 512
BLOCKS, PIECES, HALVES = K // P, N // PIECE, M // P
CHUNKS = [slice(j * PIECE, (j + 1) * PIECE) for j in range(PIECES - 1)] + [
    slice(N - PIECE, N - PIECE // 2),
    slice(N - PIECE // 2, N),
]
LANES = 16

FLOPS = 2 * K * M * N


def tile_lookup_gate_exp_relu_kernel(tc, tab, y, w, b, offs, out):
    nc = tc.nc

    tab_blocks = tab.rearrange("(p k) s -> k p s", k=BLOCKS)
    y_blocks = y.rearrange("(p k) n -> k p n", k=BLOCKS)
    out_halves = out.rearrange("(p h) n -> h p n", h=HALVES)

    with (
        tc.tile_pool(name="held", bufs=1) as held,
        tc.psum_pool(name="psum", bufs=1) as psum,
    ):
        offsets = held.tile([P, N // LANES], U16, name="offsets")
        windows = [held.tile([P, S], F32, name=f"window{k}") for k in range(BLOCKS)]
        streams = [held.tile([P, N], F32, name=f"stream{k}") for k in range(BLOCKS)]
        gates = [held.tile([P, N], F32, name=f"gate{k}") for k in range(BLOCKS)]
        xs = [held.tile([P, N], BF16, name=f"x{k}") for k in range(BLOCKS)]
        results = [held.tile([P, N], F32, name=f"result{h}") for h in range(HALVES)]
        weights = held.tile([P, BLOCKS, P, HALVES], BF16, name="weights")
        bias = held.tile([P, HALVES], F32, name="bias")
        sums = [
            [psum.tile([P, c.stop - c.start], F32, name=f"sum{i}_{h}") for h in range(HALVES)]
            for i, c in enumerate(CHUNKS)
        ]

        zero = held.tile([P, 1], F32, name="zero")
        warm = held.tile([P, 1], F32, name="warm")
        nc.vector.memset(zero[:], 0.0)
        nc.scalar.activation(warm[:], zero[:], ACT.Exp)

        nc.sync.dma_start(windows[0][:], tab_blocks[0])
        nc.sync.dma_start(offsets[:], offs)
        nc.sync.dma_start(windows[1][:], tab_blocks[1])
        nc.sync.dma_start(weights[:], w.rearrange("(p k) (q h) -> p k q h", k=BLOCKS, h=HALVES))
        nc.sync.dma_start(bias[:], b.rearrange("(p h) one -> p (h one)", h=HALVES))
        for k in range(BLOCKS):
            if k + 2 < BLOCKS:
                nc.sync.dma_start(streams[k][:], y_blocks[k])
                nc.sync.dma_start(windows[k + 2][:], tab_blocks[k + 2])
            else:
                for j in range(PIECES):
                    piece = slice(j * PIECE, (j + 1) * PIECE)
                    nc.sync.dma_start(streams[k][:, piece], y_blocks[k][:, piece])

        for k in range(BLOCKS):
            for j in range(PIECES):
                piece = slice(j * PIECE, (j + 1) * PIECE)
                piece_offsets = offsets[:, piece.start // LANES : piece.stop // LANES]
                nc.scalar.activation(gates[k][:, piece], windows[k][:].indirect(piece_offsets), ACT.Exp)
            for i, chunk in enumerate(CHUNKS):
                nc.vector.tensor_tensor(xs[k][:, chunk], gates[k][:, chunk], streams[k][:, chunk], ALU.mult)
                for h in range(HALVES):
                    nc.tensor.matmul(
                        sums[i][h][:], weights[:, k, :, h], xs[k][:, chunk], start=k == 0, stop=k == BLOCKS - 1
                    )

        for i, chunk in enumerate(CHUNKS):
            nc.vector.tensor_scalar(results[0][:, chunk], sums[i][0][:], bias[:, 0:1], 0.0, ALU.add, ALU.max)
            nc.sync.dma_start(out_halves[0][:, chunk], results[0][:, chunk])
            nc.scalar.activation(results[1][:, chunk], sums[i][1][:], ACT.Relu, bias=bias[:, 1:2])
            nc.sync.dma_start(out_halves[1][:, chunk], results[1][:, chunk])
